import numpy as np
import ml_dtypes


def mxq(x, axis, fmt="e4m3"):
    dtype, down = {"e4m3": (ml_dtypes.float8_e4m3fn, 7), "e5m2": (ml_dtypes.float8_e5m2, 14)}[fmt]
    v = np.moveaxis(np.asarray(x, np.float32).astype(ml_dtypes.bfloat16).astype(np.float64), axis, -1)
    blocks = v.reshape(v.shape[:-1] + (-1, 32))
    amax = np.abs(blocks).max(-1, keepdims=True)
    byte = np.maximum(np.where(amax > 0, np.frexp(amax)[1] - 1 + 127, 0) - down, 1)
    scale = np.exp2(byte - 127.0)
    codes = (blocks / scale).astype(np.float32).astype(dtype).astype(np.float64)
    return np.moveaxis((codes * scale).reshape(v.shape), -1, axis)


WIDE = False


def mx_kscale(k):
    if not WIDE:
        return np.ones(k)
    levels = np.array([10, -10, 5, -5, 0])
    if k % 512:
        return np.exp2(np.random.permutation(np.resize(levels, k // 32))).repeat(32)
    a = np.empty((k // 512, 16))
    for p in range(k // 512):
        a[p, :8] = np.random.permutation(np.resize(levels, 8))
        for g in range(8):
            far = levels[np.abs(levels - a[p, g]) >= 10]
            a[p, g + 8] = far[np.random.randint(len(far))]
    return np.exp2(a.ravel()).repeat(32)


def f64(x):
    return np.asarray(x).astype(np.float64)


def striped8(idx):
    return np.asarray(idx).reshape(8, -1, 16).transpose(0, 2, 1).reshape(128, -1).astype(np.uint16)


def unstriped8(offs):
    return offs.reshape(8, 16, -1).transpose(0, 2, 1).reshape(8, -1).astype(np.int64)


def pick8(x, idx, run):
    r = np.arange(len(x))
    return x[r[:, None], idx[r % (8 * run) // run]]


E2M1 = np.array([0.0, 0.5, 1.0, 1.5, 2.0, 3.0, 4.0, 6.0, -0.0, -0.5, -1.0, -1.5, -2.0, -3.0, -4.0, -6.0])


def pack_weight(w, fmt):
    k, n = w.shape
    w = f64(np.asarray(w, np.float32).astype(ml_dtypes.bfloat16)).reshape(k // 32, 32, n)
    amax = np.abs(w).max(1)
    if fmt == "e4m3":
        byte = np.frexp(amax)[1] - 1 + 127 - 7
    else:
        mant, ex = np.frexp(amax / 6.0)
        byte = np.where(mant > 0.5, ex, ex - 1) + 127
    byte = np.clip(np.where(amax > 0, byte, 1), 1, 254)
    scaled = (w * np.exp2(127.0 - byte)[:, None, :]).reshape(k, n).astype(np.float32)
    by_word = np.ascontiguousarray(scaled.reshape(k // 512, 128, 4, n).transpose(0, 1, 3, 2))
    if fmt == "e4m3":
        words = by_word.astype(ml_dtypes.float8_e4m3fn).view(np.uint8)
    else:
        c = by_word.astype(ml_dtypes.float4_e2m1fn).view(np.uint8) & 0xF
        words = (c[..., 0::2] | (c[..., 1::2] << 4)).reshape(k // 512, 128, 2 * n)
    return np.ascontiguousarray(words), np.ascontiguousarray(byte.astype(np.uint8).reshape(k // 512, 16, n))


def unpack_weight(words, scales, fmt):
    g, _, n = scales.shape
    words = np.ascontiguousarray(words).reshape(g, 128, n, -1)
    if fmt == "e4m3":
        vals = words.view(ml_dtypes.float8_e4m3fn).astype(np.float64)
    else:
        nib = np.empty((g, 128, n, 4), np.uint8)
        nib[..., 0::2] = words & 0xF
        nib[..., 1::2] = words >> 4
        vals = E2M1[nib]
    vals = vals * np.repeat(np.exp2(scales.astype(np.float64) - 127.0), 8, axis=1)[..., None]
    return vals.transpose(0, 1, 3, 2).reshape(g * 512, n)


def sgn(shape):
    return np.random.uniform(0.5, 2.0, shape) * np.where(np.random.standard_normal(shape) < 0, -1.0, 1.0)


C, D, I, Z, J, Q = 512, 512, 256, 512, 256, 128


def setup_inputs():
    n = np.random.standard_normal
    idx = np.stack([np.random.permutation(Z)[:I] for _ in range(8)])
    idx2 = np.stack([np.random.permutation(Z)[:I] for _ in range(8)])
    idx3 = np.stack([np.random.permutation(Z)[:J] for _ in range(8)])
    idx4 = np.stack([np.random.permutation(Z)[:J] for _ in range(8)])
    fc = mx_kscale(C)
    fd = mx_kscale(D)
    wpp = pack_weight(n((C, D)) * 1.0 / np.sqrt(C) * fc[:, None] / fd, "e4m3")
    oldsp = pack_weight(n((C, Z)) / fc[:, None], "e2m1")
    wkp = pack_weight(n((C, D)) * 1.0 / np.sqrt(C) * fc[:, None] / fd, "e2m1")
    newsp = pack_weight(n((C, I)) / fc[:, None], "e4m3")
    return {
        "wp_words": wpp[0],
        "wp_scales": wpp[1],
        "olds_words": oldsp[0],
        "olds_scales": oldsp[1],
        "wk_words": wkp[0],
        "wk_scales": wkp[1],
        "news_words": newsp[0],
        "news_scales": newsp[1],
        "query": (n((D, Q)) * 1.0 / np.sqrt(D) * fd[:, None]).astype(np.float32),
        "sd": (sgn((D, 1))).astype(np.float32),
        "offs": striped8(idx),
        "offs2": striped8(idx2),
        "offs3": striped8(idx3),
        "offs4": striped8(idx4),
    }


def reference(wp_words, wp_scales, olds_words, olds_scales, wk_words, wk_scales, news_words, news_scales, query, sd, offs, offs2, offs3, offs4):
    idx = unstriped8(offs)
    idx2 = unstriped8(offs2)
    idx3 = unstriped8(offs3)
    idx4 = unstriped8(offs4)
    wpu = unpack_weight(wp_words, wp_scales, "e4m3")
    oldsu = unpack_weight(olds_words, olds_scales, "e2m1")
    wku = unpack_weight(wk_words, wk_scales, "e2m1")
    newsu = unpack_weight(news_words, news_scales, "e4m3")
    kb = wpu.T @ oldsu
    kn = wku.T @ newsu
    w = pick8(kb, idx, 64) * f64(sd)
    r = kn - w
    f1 = np.zeros((D, Z))
    f1[np.arange(D)[:, None], idx2[np.arange(D) % 512 // 64]] = r
    pg = kb + f1
    queryq = mxq(f64(query), 0, "e4m3")
    pgq = mxq(pg, 0, "e4m3")
    s = queryq.T @ pgq
    y = np.maximum(pick8(s, idx3, 16), pick8(s, idx4, 16))
    return y

@@ -1,0 +1,201 @@
+from contextlib import ExitStack
+
+import concourse.mybir as mybir
+
+C, D, I, Z, J, Q = 512, 512, 256, 512, 256, 128
+FLOPS = 2 * C * D * Z + 2 * C * D * I + 2 * D * Q * Z
+
+F32 = mybir.dt.float32
+BF16 = mybir.dt.bfloat16
+I32 = mybir.dt.int32
+U32 = mybir.dt.uint32
+U16 = mybir.dt.uint16
+U8 = mybir.dt.uint8
+FP8X4 = mybir.dt.float8_e4m3fn_x4
+FP4X4 = mybir.dt.float4_e2m1fn_x4
+COPY = mybir.ActivationFunctionType.Copy
+ADD = mybir.AluOpType.add
+SUBTRACT = mybir.AluOpType.subtract
+MAX = mybir.AluOpType.max
+
+P = 128
+PACK = 4
+QUADRANTS = 4
+HALF = Z // 2
+
+
+def tile_attend_headturn_plainq_kernel(
+    tc, wp_words, wp_scales, olds_words, olds_scales, wk_words, wk_scales, news_words, news_scales,
+    query, sd, offs, offs2, offs3, offs4, out,
+):
+    nc = tc.nc
+    with ExitStack() as ctx:
+        sb = ctx.enter_context(tc.tile_pool(name="sb", bufs=1))
+        ps = ctx.enter_context(tc.psum_pool(name="ps", bufs=1))
+
+        def load_scale_rows(name, scales, width):
+            rows = sb.tile([4, QUADRANTS, width // 4], I32, name=name)
+            nc.sync.dma_start(rows[:], scales[0].rearrange("(u r) c -> r u c", r=4).bitcast(I32))
+            return rows
+
+        def zeroed_plane(name, width):
+            plane = sb.tile([P, width], U8, name=name, align_bytes=64)
+            nc.vector.memset(plane[:].bitcast(I32), 0)
+            return plane
+
+        def spread(plane, rows):
+            for u in range(QUADRANTS):
+                nc.vector.tensor_copy(plane[32 * u : 32 * u + 4, :].bitcast(I32), rows[:, u, :])
+
+        def load_list(name, source):
+            offsets = sb.tile([P, source.shape[1]], U16, name=name)
+            nc.sync.dma_start(offsets[:], source)
+            return offsets
+
+        wp_rows = load_scale_rows("wp_rows", wp_scales, D)
+        olds_rows = load_scale_rows("olds_rows", olds_scales, Z)
+        wp_raw = sb.tile([P, D], U32, name="wp_raw")
+        nc.sync.dma_start(wp_raw[:].bitcast(I32), wp_words[0].rearrange("p n t -> p (n t)").bitcast(I32))
+        olds_codes = sb.tile([P, 2 * Z], U8, name="olds_codes", align_bytes=64)
+        nc.sync.dma_start(olds_codes[:].bitcast(I32), olds_words[0].bitcast(I32))
+        wk_rows = load_scale_rows("wk_rows", wk_scales, D)
+        news_rows = load_scale_rows("news_rows", news_scales, I)
+        wk_raw = sb.tile([P, 2 * D], U8, name="wk_raw")
+        nc.sync.dma_start(wk_raw[:].bitcast(I32), wk_words[0].bitcast(I32))
+        news_codes = sb.tile([P, I], U32, name="news_codes", align_bytes=64)
+        nc.sync.dma_start(news_codes[:].bitcast(I32), news_words[0].rearrange("p n t -> p (n t)").bitcast(I32))
+        fetch_list = load_list("fetch_list", offs)
+        sd_cols = sb.tile([P, PACK], F32, name="sd_cols")
+        nc.sync.dma_start(sd_cols[:], sd.rearrange("(p t) o -> p (t o)", t=PACK))
+        put_list = load_list("put_list", offs2)
+        query_raw = sb.tile([P, PACK, Q], F32, name="query_raw")
+        nc.sync.dma_start(query_raw[:], query.rearrange("(p t) q -> p t q", t=PACK))
+        pick_list_a = load_list("pick_list_a", offs3)
+        pick_list_b = load_list("pick_list_b", offs4)
+
+        wp_spread = zeroed_plane("wp_spread", D)
+        olds_plane = zeroed_plane("olds_plane", Z)
+        wk_spread = zeroed_plane("wk_spread", D)
+        news_plane = zeroed_plane("news_plane", I)
+        f1 = [sb.tile([P, Z], F32, name="f1_%d" % t) for t in range(PACK)]
+        for t in range(PACK):
+            nc.vector.memset(f1[t][:], 0.0)
+
+        spread(wp_spread, wp_rows)
+        spread(olds_plane, olds_rows)
+        wp_plane = [sb.tile([P, P], U8, name="wp_plane_%d" % t, align_bytes=64) for t in range(PACK)]
+        wp_codes = [sb.tile([P, P], U32, name="wp_codes_%d" % t, align_bytes=64) for t in range(PACK)]
+        for t in range(PACK):
+            nc.vector.tensor_copy(wp_plane[t][:], wp_spread[:, t : D : PACK])
+            nc.scalar.copy(wp_codes[t][:], wp_raw[:, t : D : PACK])
+
+        def kb_product(bank, t, z0, z1):
+            nc.tensor.matmul_mx(
+                out=bank,
+                lhsT=wp_codes[t][:].bitcast(FP8X4),
+                lhsT_scale=wp_plane[t][:],
+                rhs=olds_codes[:, 2 * z0 : 2 * z1].bitcast(FP4X4),
+                rhs_scale=olds_plane[:, z0:z1],
+                start=True,
+                stop=True,
+            )
+
+        kb = [sb.tile([P, Z], F32, name="kb_%d" % t) for t in range(PACK)]
+        kb_first_low = ps.tile([P, HALF], F32, name="kb_first_low")
+        kb_first_high = ps.tile([P, HALF], F32, name="kb_first_high")
+        kb_product(kb_first_low[:], 0, 0, HALF)
+        kb_product(kb_first_high[:], 0, HALF, Z)
+        kb_banks = [kb_first_low] + [ps.tile([P, Z], F32, name="kb_bank_%d" % t) for t in range(1, PACK)]
+        for t in range(1, PACK):
+            kb_product(kb_banks[t][:], t, 0, Z)
+
+        spread(wk_spread, wk_rows)
+        spread(news_plane, news_rows)
+        nc.scalar.copy(kb[0][:, :HALF], kb_first_low[:])
+        nc.vector.tensor_copy(kb[0][:, HALF:], kb_first_high[:])
+        nc.vector.tensor_copy(kb[1][:], kb_banks[1][:])
+        wk_plane = sb.tile([P, D], U8, name="wk_plane", align_bytes=64)
+        nc.vector.tensor_copy(
+            wk_plane[:].rearrange("p (t m) -> p m t", t=PACK), wk_spread[:].rearrange("p (m t) -> p m t", t=PACK)
+        )
+        wk_codes = sb.tile([P, 2 * D], U8, name="wk_codes", align_bytes=64)
+        nc.vector.tensor_copy(
+            wk_codes[:].bitcast(U16).rearrange("p (t m) -> p m t", t=PACK),
+            wk_raw[:].bitcast(U16).rearrange("p (m t) -> p m t", t=PACK),
+        )
+        kn_banks = [ps.tile([P, 2, I], F32, name="kn_bank_%d" % b, tag="late_%d" % b) for b in range(2)]
+        for t in range(PACK):
+            nc.tensor.matmul_mx(
+                out=kn_banks[t // 2][:, t % 2, :],
+                lhsT=wk_codes[:, 2 * P * t : 2 * P * (t + 1)].bitcast(FP4X4),
+                lhsT_scale=wk_plane[:, P * t : P * (t + 1)],
+                rhs=news_codes[:].bitcast(FP8X4),
+                rhs_scale=news_plane[:],
+                start=True,
+                stop=True,
+            )
+
+        w = [sb.tile([P, I], F32, name="w_%d" % t) for t in range(PACK)]
+        r = [sb.tile([P, I], F32, name="r_%d" % t) for t in range(PACK)]
+        pg_low = sb.tile([P, HALF, PACK], BF16, name="pg_low", align_bytes=64)
+        pg_high = sb.tile([P, HALF, PACK], BF16, name="pg_high", align_bytes=64)
+
+        def fetch(t):
+            nc.scalar.activation(w[t][:], kb[t][:].indirect(fetch_list[:]), COPY, scale=sd_cols[:, t : t + 1])
+            nc.vector.tensor_tensor(r[t][:], kn_banks[t // 2][:, t % 2, :], w[t][:], SUBTRACT)
+
+        def put(t):
+            nc.scalar.activation(f1[t][:].indirect(put_list[:]), r[t][:], COPY)
+
+        def add(t):
+            nc.vector.tensor_tensor(pg_low[:, :, t], kb_banks[t][:, :HALF], f1[t][:, :HALF], ADD)
+            nc.gpsimd.tensor_tensor(pg_high[:, :, t], kb[t][:, HALF:], f1[t][:, HALF:], ADD)
+
+        fetch(0)
+        fetch(1)
+        put(0)
+        nc.vector.tensor_copy(kb[2][:], kb_banks[2][:])
+        nc.vector.tensor_copy(kb[3][:], kb_banks[3][:])
+        fetch(2)
+        put(1)
+        fetch(3)
+        add(0)
+
+        query_grouped = sb.tile([P, Q, PACK], BF16, name="query_grouped", align_bytes=64)
+        nc.vector.tensor_copy(query_grouped[:], query_raw[:].rearrange("p t q -> p q t"))
+        put(2)
+        add(1)
+        query_codes = sb.tile([P, Q], U32, name="query_codes", align_bytes=64)
+        query_plane = sb.tile([P, Q], U8, name="query_plane", align_bytes=64)
+        nc.vector.quantize_mx(
+            query_codes[:].bitcast(FP8X4), query_plane[:], query_grouped[:].rearrange("p q t -> p (q t)")
+        )
+        put(3)
+        add(2)
+        add(3)
+
+        s = sb.tile([P, Z], F32, name="s")
+        s_banks = [ps.tile([P, HALF], F32, name="s_bank_%d" % b, tag="late_%d" % b) for b in range(2)]
+        for b, pg in enumerate((pg_low, pg_high)):
+            pg_codes = sb.tile([P, HALF], U32, name="pg_codes_%d" % b, align_bytes=64)
+            pg_plane = sb.tile([P, HALF], U8, name="pg_plane_%d" % b, align_bytes=64)
+            nc.vector.quantize_mx(pg_codes[:].bitcast(FP8X4), pg_plane[:], pg[:].rearrange("p z t -> p (z t)"))
+            nc.tensor.matmul_mx(
+                out=s_banks[b][:],
+                lhsT=query_codes[:].bitcast(FP8X4),
+                lhsT_scale=query_plane[:],
+                rhs=pg_codes[:].bitcast(FP8X4),
+                rhs_scale=pg_plane[:],
+                start=True,
+                stop=True,
+            )
+        nc.scalar.copy(s[:, :HALF], s_banks[0][:])
+        nc.vector.tensor_copy(s[:, HALF:], s_banks[1][:])
+
+        picked_a = sb.tile([P, J], F32, name="picked_a")
+        picked_b = sb.tile([P, J], F32, name="picked_b")
+        nc.scalar.activation(picked_a[:], s[:].indirect(pick_list_a[:]), COPY)
+        nc.vector.tensor_copy(picked_b[:], s[:].indirect(pick_list_b[:]))
+        larger = sb.tile([P, J], F32, name="larger")
+        nc.vector.tensor_tensor(larger[:], picked_a[:], picked_b[:], MAX)
+        nc.sync.dma_start(out, larger[:])

@@ -18,10 +18,13 @@ ADD = mybir.AluOpType.add
 SUBTRACT = mybir.AluOpType.subtract
 MAX = mybir.AluOpType.max
 
+mybir_bytes = {U32: 4, U16: 2, U8: 1}
 P = 128
 PACK = 4
 QUADRANTS = 4
 HALF = Z // 2
+PIECES = 4
+PIECE = Z // PIECES
 
 
 def tile_attend_headturn_plainq_kernel(
@@ -33,67 +36,81 @@ def tile_attend_headturn_plainq_kernel(
         sb = ctx.enter_context(tc.tile_pool(name="sb", bufs=1))
         ps = ctx.enter_context(tc.psum_pool(name="ps", bufs=1))
 
-        def load_scale_rows(name, scales, width):
-            rows = sb.tile([4, QUADRANTS, width // 4], I32, name=name)
-            nc.sync.dma_start(rows[:], scales[0].rearrange("(u r) c -> r u c", r=4).bitcast(I32))
+        def load_scale_rows(filler, queue, name, scales, width):
+            rows = sb.tile([P, 2, width], U8, name=name, align_bytes=64)
+            filler.memset(rows[:].bitcast(I32), 0)
+            by_quadrant = scales[0].rearrange("(h l r) c -> l r h c", h=2, l=2).bitcast(I32)
+            for low in range(2):
+                queue.dma_start(rows[32 * low : 32 * low + 4].bitcast(I32), by_quadrant[low])
             return rows
 
-        def zeroed_plane(name, width):
+        def load_plane(name, scales, width):
             plane = sb.tile([P, width], U8, name=name, align_bytes=64)
             nc.vector.memset(plane[:].bitcast(I32), 0)
+            for u in range(QUADRANTS):
+                nc.sync.dma_start(plane[32 * u : 32 * u + 4, :].bitcast(I32), scales[0, 4 * u : 4 * u + 4, :].bitcast(I32))
             return plane
 
-        def spread(plane, rows):
-            for u in range(QUADRANTS):
-                nc.vector.tensor_copy(plane[32 * u : 32 * u + 4, :].bitcast(I32), rows[:, u, :])
+        def spread(rows):
+            nc.vector.tensor_copy(rows[P // 2 :, 0, :].bitcast(I32), rows[: P // 2, 1, :].bitcast(I32))
+            return rows[:, 0, :]
+
+        def deal(copy, dealt, given, first, last):
+            run = 16 // mybir_bytes[given.dtype]
+            copy(
+                dealt.rearrange("p (t c i) -> p c t i", t=PACK, i=run)[:, :, first:last, :],
+                given.rearrange("p (c i t) -> p c t i", t=PACK, i=run)[:, :, first:last, :],
+            )
 
         def load_list(name, source):
             offsets = sb.tile([P, source.shape[1]], U16, name=name)
             nc.sync.dma_start(offsets[:], source)
             return offsets
 
-        wp_rows = load_scale_rows("wp_rows", wp_scales, D)
-        olds_rows = load_scale_rows("olds_rows", olds_scales, Z)
+        wk_rows = sb.tile([4, QUADRANTS, D // 4], I32, name="wk_rows")
+        nc.scalar.dma_start(wk_rows[:], wk_scales[0].rearrange("(u r) c -> r u c", r=4).bitcast(I32))
         wp_raw = sb.tile([P, D], U32, name="wp_raw")
         nc.sync.dma_start(wp_raw[:].bitcast(I32), wp_words[0].rearrange("p n t -> p (n t)").bitcast(I32))
         olds_codes = sb.tile([P, 2 * Z], U8, name="olds_codes", align_bytes=64)
         nc.sync.dma_start(olds_codes[:].bitcast(I32), olds_words[0].bitcast(I32))
-        wk_rows = load_scale_rows("wk_rows", wk_scales, D)
-        news_rows = load_scale_rows("news_rows", news_scales, I)
+        olds_rows = load_scale_rows(nc.gpsimd, nc.sync, "olds_rows", olds_scales, Z)
+        wp_rows = load_scale_rows(nc.vector, nc.scalar, "wp_rows", wp_scales, D)
         wk_raw = sb.tile([P, 2 * D], U8, name="wk_raw")
         nc.sync.dma_start(wk_raw[:].bitcast(I32), wk_words[0].bitcast(I32))
-        news_codes = sb.tile([P, I], U32, name="news_codes", align_bytes=64)
-        nc.sync.dma_start(news_codes[:].bitcast(I32), news_words[0].rearrange("p n t -> p (n t)").bitcast(I32))
+        wk_spread = sb.tile([P, D], U8, name="wk_spread")
+        nc.vector.memset(wk_spread[:].bitcast(I32), 0)
         fetch_list = load_list("fetch_list", offs)
         sd_cols = sb.tile([P, PACK], F32, name="sd_cols")
         nc.sync.dma_start(sd_cols[:], sd.rearrange("(p t) o -> p (t o)", t=PACK))
+        news_codes = sb.tile([P, I], U32, name="news_codes", align_bytes=64)
+        nc.sync.dma_start(news_codes[:].bitcast(I32), news_words[0].rearrange("p n t -> p (n t)").bitcast(I32))
+        news_plane = load_plane("news_plane", news_scales, I)
         put_list = load_list("put_list", offs2)
-        query_raw = sb.tile([P, PACK, Q], F32, name="query_raw")
-        nc.sync.dma_start(query_raw[:], query.rearrange("(p t) q -> p t q", t=PACK))
         pick_list_a = load_list("pick_list_a", offs3)
         pick_list_b = load_list("pick_list_b", offs4)
 
-        wp_spread = zeroed_plane("wp_spread", D)
-        olds_plane = zeroed_plane("olds_plane", Z)
-        wk_spread = zeroed_plane("wk_spread", D)
-        news_plane = zeroed_plane("news_plane", I)
         f1 = [sb.tile([P, Z], F32, name="f1_%d" % t) for t in range(PACK)]
         for t in range(PACK):
             nc.vector.memset(f1[t][:], 0.0)
 
-        spread(wp_spread, wp_rows)
-        spread(olds_plane, olds_rows)
-        wp_plane = [sb.tile([P, P], U8, name="wp_plane_%d" % t, align_bytes=64) for t in range(PACK)]
-        wp_codes = [sb.tile([P, P], U32, name="wp_codes_%d" % t, align_bytes=64) for t in range(PACK)]
-        for t in range(PACK):
-            nc.vector.tensor_copy(wp_plane[t][:], wp_spread[:, t : D : PACK])
-            nc.scalar.copy(wp_codes[t][:], wp_raw[:, t : D : PACK])
+        for u in (0, 1, 3, 2):
+            nc.vector.tensor_copy(wk_spread[32 * u : 32 * u + 4, :].bitcast(I32), wk_rows[:, u, :])
+        wp_spread = spread(wp_rows)
+        olds_plane = spread(olds_rows)
+        wp_plane = sb.tile([P, D], U8, name="wp_plane", align_bytes=64)
+        wp_codes = sb.tile([P, D], U32, name="wp_codes", align_bytes=64)
+        for first, last in ((0, 1), (1, PACK)):
+            deal(nc.vector.tensor_copy, wp_plane[:], wp_spread, first, last)
+            deal(nc.scalar.copy, wp_codes[:], wp_raw[:], first, last)
+
+        query_raw = sb.tile([P, PACK, Q], F32, name="query_raw", tag="wp_raw")
+        nc.sync.dma_start(query_raw[:], query.rearrange("(p t) q -> p t q", t=PACK))
 
         def kb_product(bank, t, z0, z1):
             nc.tensor.matmul_mx(
                 out=bank,
-                lhsT=wp_codes[t][:].bitcast(FP8X4),
-                lhsT_scale=wp_plane[t][:],
+                lhsT=wp_codes[:, P * t : P * (t + 1)].bitcast(FP8X4),
+                lhsT_scale=wp_plane[:, P * t : P * (t + 1)],
                 rhs=olds_codes[:, 2 * z0 : 2 * z1].bitcast(FP4X4),
                 rhs_scale=olds_plane[:, z0:z1],
                 start=True,
@@ -101,32 +118,27 @@ def tile_attend_headturn_plainq_kernel(
             )
 
         kb = [sb.tile([P, Z], F32, name="kb_%d" % t) for t in range(PACK)]
-        kb_first_low = ps.tile([P, HALF], F32, name="kb_first_low")
-        kb_first_high = ps.tile([P, HALF], F32, name="kb_first_high")
-        kb_product(kb_first_low[:], 0, 0, HALF)
-        kb_product(kb_first_high[:], 0, HALF, Z)
-        kb_banks = [kb_first_low] + [ps.tile([P, Z], F32, name="kb_bank_%d" % t) for t in range(1, PACK)]
+        first_cuts = (0, HALF, HALF + PIECE, Z)
+        first_banks = [ps.tile([P, z1 - z0], F32, name="kb_first_%d" % n) for n, (z0, z1) in enumerate(zip(first_cuts, first_cuts[1:]))]
+        for bank, z0, z1 in zip(first_banks, first_cuts, first_cuts[1:]):
+            kb_product(bank[:], 0, z0, z1)
+        kb_banks = {t: ps.tile([P, Z], F32, name="kb_bank_%d" % t) for t in range(1, PACK)}
         for t in range(1, PACK):
             kb_product(kb_banks[t][:], t, 0, Z)
 
-        spread(wk_spread, wk_rows)
-        spread(news_plane, news_rows)
-        nc.scalar.copy(kb[0][:, :HALF], kb_first_low[:])
-        nc.vector.tensor_copy(kb[0][:, HALF:], kb_first_high[:])
-        nc.vector.tensor_copy(kb[1][:], kb_banks[1][:])
-        wk_plane = sb.tile([P, D], U8, name="wk_plane", align_bytes=64)
-        nc.vector.tensor_copy(
-            wk_plane[:].rearrange("p (t m) -> p m t", t=PACK), wk_spread[:].rearrange("p (m t) -> p m t", t=PACK)
-        )
         wk_codes = sb.tile([P, 2 * D], U8, name="wk_codes", align_bytes=64)
-        nc.vector.tensor_copy(
-            wk_codes[:].bitcast(U16).rearrange("p (t m) -> p m t", t=PACK),
-            wk_raw[:].bitcast(U16).rearrange("p (m t) -> p m t", t=PACK),
-        )
-        kn_banks = [ps.tile([P, 2, I], F32, name="kn_bank_%d" % b, tag="late_%d" % b) for b in range(2)]
-        for t in range(PACK):
+        deal(nc.scalar.copy, wk_codes[:].bitcast(U16), wk_raw[:].bitcast(U16), 0, PACK)
+        for copy, bank, z0, z1 in zip((nc.scalar.copy, nc.vector.tensor_copy, nc.vector.tensor_copy), first_banks, first_cuts, first_cuts[1:]):
+            copy(kb[0][:, z0:z1], bank[:])
+        wk_plane = sb.tile([P, D], U8, name="wk_plane", tag="wp_rows", align_bytes=64)
+        deal(nc.vector.tensor_copy, wk_plane[:], wk_spread[:], 0, PACK)
+        for t in range(1, PACK):
+            nc.vector.tensor_copy(kb[t][:], kb_banks[t][:])
+
+        def kn_product(t):
+            kn = ps.tile([P, I], F32, name="kn_%d" % t, tag="late_%d" % (t % 2))
             nc.tensor.matmul_mx(
-                out=kn_banks[t // 2][:, t % 2, :],
+                out=kn[:],
                 lhsT=wk_codes[:, 2 * P * t : 2 * P * (t + 1)].bitcast(FP4X4),
                 lhsT_scale=wk_plane[:, P * t : P * (t + 1)],
                 rhs=news_codes[:].bitcast(FP8X4),
@@ -134,54 +146,57 @@ def tile_attend_headturn_plainq_kernel(
                 start=True,
                 stop=True,
             )
+            return kn
 
         w = [sb.tile([P, I], F32, name="w_%d" % t) for t in range(PACK)]
         r = [sb.tile([P, I], F32, name="r_%d" % t) for t in range(PACK)]
-        pg_low = sb.tile([P, HALF, PACK], BF16, name="pg_low", align_bytes=64)
-        pg_high = sb.tile([P, HALF, PACK], BF16, name="pg_high", align_bytes=64)
-
-        def fetch(t):
+        for t in range(PACK):
             nc.scalar.activation(w[t][:], kb[t][:].indirect(fetch_list[:]), COPY, scale=sd_cols[:, t : t + 1])
-            nc.vector.tensor_tensor(r[t][:], kn_banks[t // 2][:, t % 2, :], w[t][:], SUBTRACT)
+        for t in range(PACK):
+            nc.vector.tensor_tensor(r[t][:], kn_product(t)[:], w[t][:], SUBTRACT)
+
+        pg_pair = [sb.tile([P, 2, Z], BF16, name="pg_pair_%d" % u) for u in range(2)]
+        pg = [sb.tile([P, PIECE, PACK], BF16, name="pg_%d" % k, align_bytes=64) for k in range(PIECES)]
 
         def put(t):
             nc.scalar.activation(f1[t][:].indirect(put_list[:]), r[t][:], COPY)
 
-        def add(t):
-            nc.vector.tensor_tensor(pg_low[:, :, t], kb_banks[t][:, :HALF], f1[t][:, :HALF], ADD)
-            nc.gpsimd.tensor_tensor(pg_high[:, :, t], kb[t][:, HALF:], f1[t][:, HALF:], ADD)
+        def add(t, z0, z1):
+            nc.vector.tensor_tensor(pg_pair[t // 2][:, t % 2, z0:z1], kb[t][:, z0:z1], f1[t][:, z0:z1], ADD)
 
-        fetch(0)
-        fetch(1)
+        def weave(copy, u, k):
+            copy(pg[k][:, :, 2 * u : 2 * u + 2], pg_pair[u][:, :, PIECE * k : PIECE * (k + 1)].rearrange("p e z -> p z e"))
+
         put(0)
-        nc.vector.tensor_copy(kb[2][:], kb_banks[2][:])
-        nc.vector.tensor_copy(kb[3][:], kb_banks[3][:])
-        fetch(2)
-        put(1)
-        fetch(3)
-        add(0)
-
         query_grouped = sb.tile([P, Q, PACK], BF16, name="query_grouped", align_bytes=64)
         nc.vector.tensor_copy(query_grouped[:], query_raw[:].rearrange("p t q -> p q t"))
-        put(2)
-        add(1)
         query_codes = sb.tile([P, Q], U32, name="query_codes", align_bytes=64)
         query_plane = sb.tile([P, Q], U8, name="query_plane", align_bytes=64)
         nc.vector.quantize_mx(
             query_codes[:].bitcast(FP8X4), query_plane[:], query_grouped[:].rearrange("p q t -> p (q t)")
         )
+        add(0, 0, Z)
+        put(1)
+        add(1, 0, Z)
+        for k in range(PIECES):
+            weave(nc.vector.tensor_copy, 0, k)
+        put(2)
+        add(2, 0, Z)
         put(3)
-        add(2)
-        add(3)
+        for k in range(PIECES):
+            add(3, PIECE * k, PIECE * (k + 1))
+        for k in range(PIECES):
+            weave(nc.scalar.copy if k < PIECES // 2 else nc.vector.tensor_copy, 1, k)
 
         s = sb.tile([P, Z], F32, name="s")
-        s_banks = [ps.tile([P, HALF], F32, name="s_bank_%d" % b, tag="late_%d" % b) for b in range(2)]
-        for b, pg in enumerate((pg_low, pg_high)):
-            pg_codes = sb.tile([P, HALF], U32, name="pg_codes_%d" % b, align_bytes=64)
-            pg_plane = sb.tile([P, HALF], U8, name="pg_plane_%d" % b, align_bytes=64)
-            nc.vector.quantize_mx(pg_codes[:].bitcast(FP8X4), pg_plane[:], pg[:].rearrange("p z t -> p (z t)"))
+        s_banks = [ps.tile([P, PIECE], F32, name="s_bank_%d" % k, tag=tag) for k, tag in enumerate(("late_0", "late_1", "kb_first_0", "kb_first_1"))]
+        order = (0, 2, 3, 1)
+        for k in order:
+            pg_codes = sb.tile([P, PIECE], U32, name="pg_codes_%d" % k, align_bytes=64)
+            pg_plane = sb.tile([P, PIECE], U8, name="pg_plane_%d" % k, align_bytes=64)
+            nc.vector.quantize_mx(pg_codes[:].bitcast(FP8X4), pg_plane[:], pg[k][:].rearrange("p z t -> p (z t)"))
             nc.tensor.matmul_mx(
-                out=s_banks[b][:],
+                out=s_banks[k][:],
                 lhsT=query_codes[:].bitcast(FP8X4),
                 lhsT_scale=query_plane[:],
                 rhs=pg_codes[:].bitcast(FP8X4),
@@ -189,13 +204,17 @@ def tile_attend_headturn_plainq_kernel(
                 start=True,
                 stop=True,
             )
-        nc.scalar.copy(s[:, :HALF], s_banks[0][:])
-        nc.vector.tensor_copy(s[:, HALF:], s_banks[1][:])
+        for n, k in enumerate(order):
+            copy = nc.scalar.copy if n < PIECES - 1 else nc.vector.tensor_copy
+            copy(s[:, PIECE * k : PIECE * (k + 1)], s_banks[k][:])
 
         picked_a = sb.tile([P, J], F32, name="picked_a")
         picked_b = sb.tile([P, J], F32, name="picked_b")
-        nc.scalar.activation(picked_a[:], s[:].indirect(pick_list_a[:]), COPY)
-        nc.vector.tensor_copy(picked_b[:], s[:].indirect(pick_list_b[:]))
         larger = sb.tile([P, J], F32, name="larger")
-        nc.vector.tensor_tensor(larger[:], picked_a[:], picked_b[:], MAX)
-        nc.sync.dma_start(out, larger[:])
+        halves = [(slice(J // 2 * h, J // 2 * (h + 1)), slice(J // 32 * h, J // 32 * (h + 1))) for h in range(2)]
+        for picks, columns in halves:
+            nc.scalar.activation(picked_a[:, picks], s[:].indirect(pick_list_a[:, columns]), COPY)
+            nc.vector.tensor_copy(picked_b[:, picks], s[:].indirect(pick_list_b[:, columns]))
+        for (picks, columns), queue in zip(halves, (nc.sync, nc.scalar)):
+            nc.vector.tensor_tensor(larger[:, picks], picked_a[:, picks], picked_b[:, picks], MAX)
+            queue.dma_start(out[:, picks], larger[:, picks])

@@ -36,29 +36,30 @@ def tile_attend_headturn_plainq_kernel(
         sb = ctx.enter_context(tc.tile_pool(name="sb", bufs=1))
         ps = ctx.enter_context(tc.psum_pool(name="ps", bufs=1))
 
-        def load_scale_rows(filler, queue, name, scales, width):
+        def load_scale_rows(filler, name, scales, width):
             rows = sb.tile([P, 2, width], U8, name=name, align_bytes=64)
             filler.memset(rows[:].bitcast(I32), 0)
             by_quadrant = scales[0].rearrange("(h l r) c -> l r h c", h=2, l=2).bitcast(I32)
             for low in range(2):
-                queue.dma_start(rows[32 * low : 32 * low + 4].bitcast(I32), by_quadrant[low])
+                nc.sync.dma_start(rows[32 * low : 32 * low + 4].bitcast(I32), by_quadrant[low])
             return rows
 
-        def load_plane(name, scales, width):
-            plane = sb.tile([P, width], U8, name=name, align_bytes=64)
-            nc.vector.memset(plane[:].bitcast(I32), 0)
-            for u in range(QUADRANTS):
-                nc.sync.dma_start(plane[32 * u : 32 * u + 4, :].bitcast(I32), scales[0, 4 * u : 4 * u + 4, :].bitcast(I32))
-            return plane
-
-        def spread(rows):
+        def complete_plane(rows):
             nc.vector.tensor_copy(rows[P // 2 :, 0, :].bitcast(I32), rows[: P // 2, 1, :].bitcast(I32))
             return rows[:, 0, :]
+
+        def zeroed_plane(name, width):
+            plane = sb.tile([P, width], U8, name=name, align_bytes=64)
+            nc.vector.memset(plane[:].bitcast(I32), 0)
+            return plane
+
+        def spread(copy, plane, rows, u):
+            copy(plane[32 * u : 32 * u + 4, :].bitcast(U32), rows[:, u, :])
 
         def deal(copy, dealt, given, first, last):
             run = 16 // mybir_bytes[given.dtype]
             copy(
-                dealt.rearrange("p (t c i) -> p c t i", t=PACK, i=run)[:, :, first:last, :],
+                dealt.rearrange("p (t c i) -> p c t i", t=last - first, i=run),
                 given.rearrange("p (c i t) -> p c t i", t=PACK, i=run)[:, :, first:last, :],
             )
 
@@ -67,41 +68,45 @@ def tile_attend_headturn_plainq_kernel(
             nc.sync.dma_start(offsets[:], source)
             return offsets
 
-        wk_rows = sb.tile([4, QUADRANTS, D // 4], I32, name="wk_rows")
-        nc.scalar.dma_start(wk_rows[:], wk_scales[0].rearrange("(u r) c -> r u c", r=4).bitcast(I32))
         wp_raw = sb.tile([P, D], U32, name="wp_raw")
         nc.sync.dma_start(wp_raw[:].bitcast(I32), wp_words[0].rearrange("p n t -> p (n t)").bitcast(I32))
+        wp_rows = load_scale_rows(nc.gpsimd, "wp_rows", wp_scales, D)
         olds_codes = sb.tile([P, 2 * Z], U8, name="olds_codes", align_bytes=64)
         nc.sync.dma_start(olds_codes[:].bitcast(I32), olds_words[0].bitcast(I32))
-        olds_rows = load_scale_rows(nc.gpsimd, nc.sync, "olds_rows", olds_scales, Z)
-        wp_rows = load_scale_rows(nc.vector, nc.scalar, "wp_rows", wp_scales, D)
+        olds_rows = load_scale_rows(nc.vector, "olds_rows", olds_scales, Z)
+        wk_rows = sb.tile([4, QUADRANTS, D // 4], U32, name="wk_rows")
+        nc.sync.dma_start(wk_rows[:].bitcast(I32), wk_scales[0].rearrange("(u r) c -> r u c", r=4).bitcast(I32))
         wk_raw = sb.tile([P, 2 * D], U8, name="wk_raw")
         nc.sync.dma_start(wk_raw[:].bitcast(I32), wk_words[0].bitcast(I32))
-        wk_spread = sb.tile([P, D], U8, name="wk_spread")
-        nc.vector.memset(wk_spread[:].bitcast(I32), 0)
         fetch_list = load_list("fetch_list", offs)
         sd_cols = sb.tile([P, PACK], F32, name="sd_cols")
         nc.sync.dma_start(sd_cols[:], sd.rearrange("(p t) o -> p (t o)", t=PACK))
+        news_plane = zeroed_plane("news_plane", I)
+        wk_spread = zeroed_plane("wk_spread", D)
         news_codes = sb.tile([P, I], U32, name="news_codes", align_bytes=64)
         nc.sync.dma_start(news_codes[:].bitcast(I32), news_words[0].rearrange("p n t -> p (n t)").bitcast(I32))
-        news_plane = load_plane("news_plane", news_scales, I)
+        for u in range(QUADRANTS):
+            nc.sync.dma_start(
+                news_plane[32 * u : 32 * u + 4, :].bitcast(I32), news_scales[0, 4 * u : 4 * u + 4, :].bitcast(I32)
+            )
         put_list = load_list("put_list", offs2)
         pick_list_a = load_list("pick_list_a", offs3)
         pick_list_b = load_list("pick_list_b", offs4)
 
         f1 = [sb.tile([P, Z], F32, name="f1_%d" % t) for t in range(PACK)]
         for t in range(PACK):
-            nc.vector.memset(f1[t][:], 0.0)
+            (nc.vector if t < 2 else nc.gpsimd).memset(f1[t][:], 0.0)
 
-        for u in (0, 1, 3, 2):
-            nc.vector.tensor_copy(wk_spread[32 * u : 32 * u + 4, :].bitcast(I32), wk_rows[:, u, :])
-        wp_spread = spread(wp_rows)
-        olds_plane = spread(olds_rows)
-        wp_plane = sb.tile([P, D], U8, name="wp_plane", align_bytes=64)
-        wp_codes = sb.tile([P, D], U32, name="wp_codes", align_bytes=64)
+        wp_spread = complete_plane(wp_rows)
+        olds_plane = complete_plane(olds_rows)
+        wp_plane, wp_codes = [], []
         for first, last in ((0, 1), (1, PACK)):
-            deal(nc.vector.tensor_copy, wp_plane[:], wp_spread, first, last)
-            deal(nc.scalar.copy, wp_codes[:], wp_raw[:], first, last)
+            plane = sb.tile([P, P * (last - first)], U8, name="wp_plane_%d" % first, align_bytes=64)
+            codes = sb.tile([P, P * (last - first)], U32, name="wp_codes_%d" % first, align_bytes=64)
+            deal(nc.vector.tensor_copy, plane[:], wp_spread, first, last)
+            deal(nc.scalar.copy, codes[:], wp_raw[:], first, last)
+            wp_plane.extend(plane[:, P * n : P * (n + 1)] for n in range(last - first))
+            wp_codes.extend(codes[:, P * n : P * (n + 1)] for n in range(last - first))
 
         query_raw = sb.tile([P, PACK, Q], F32, name="query_raw", tag="wp_raw")
         nc.sync.dma_start(query_raw[:], query.rearrange("(p t) q -> p t q", t=PACK))
@@ -109,8 +114,8 @@ def tile_attend_headturn_plainq_kernel(
         def kb_product(bank, t, z0, z1):
             nc.tensor.matmul_mx(
                 out=bank,
-                lhsT=wp_codes[:, P * t : P * (t + 1)].bitcast(FP8X4),
-                lhsT_scale=wp_plane[:, P * t : P * (t + 1)],
+                lhsT=wp_codes[t].bitcast(FP8X4),
+                lhsT_scale=wp_plane[t],
                 rhs=olds_codes[:, 2 * z0 : 2 * z1].bitcast(FP4X4),
                 rhs_scale=olds_plane[:, z0:z1],
                 start=True,
@@ -130,10 +135,13 @@ def tile_attend_headturn_plainq_kernel(
         deal(nc.scalar.copy, wk_codes[:].bitcast(U16), wk_raw[:].bitcast(U16), 0, PACK)
         for copy, bank, z0, z1 in zip((nc.scalar.copy, nc.vector.tensor_copy, nc.vector.tensor_copy), first_banks, first_cuts, first_cuts[1:]):
             copy(kb[0][:, z0:z1], bank[:])
-        wk_plane = sb.tile([P, D], U8, name="wk_plane", tag="wp_rows", align_bytes=64)
-        deal(nc.vector.tensor_copy, wk_plane[:], wk_spread[:], 0, PACK)
+        for u in range(QUADRANTS):
+            spread(nc.gpsimd.tensor_copy if u == 0 else nc.vector.tensor_copy, wk_spread, wk_rows, u)
         for t in range(1, PACK):
             nc.vector.tensor_copy(kb[t][:], kb_banks[t][:])
+        wk_plane = sb.tile([P, D], U8, name="wk_plane", align_bytes=64)
+        for t in range(PACK):
+            deal(nc.gpsimd.tensor_copy, wk_plane[:, P * t : P * (t + 1)], wk_spread[:], t, t + 1)
 
         def kn_product(t):
             kn = ps.tile([P, I], F32, name="kn_%d" % t, tag="late_%d" % (t % 2))
@@ -183,14 +191,14 @@ def tile_attend_headturn_plainq_kernel(
         put(2)
         add(2, 0, Z)
         put(3)
-        for k in range(PIECES):
+        for k in (0, 2, 3, 1):
             add(3, PIECE * k, PIECE * (k + 1))
         for k in range(PIECES):
             weave(nc.scalar.copy if k < PIECES // 2 else nc.vector.tensor_copy, 1, k)
 
         s = sb.tile([P, Z], F32, name="s")
         s_banks = [ps.tile([P, PIECE], F32, name="s_bank_%d" % k, tag=tag) for k, tag in enumerate(("late_0", "late_1", "kb_first_0", "kb_first_1"))]
-        order = (0, 2, 3, 1)
+        order = (2, 0, 3, 1)
         for k in order:
             pg_codes = sb.tile([P, PIECE], U32, name="pg_codes_%d" % k, align_bytes=64)
             pg_plane = sb.tile([P, PIECE], U8, name="pg_plane_%d" % k, align_bytes=64)

from contextlib import ExitStack

import concourse.mybir as mybir

C, D, I, Z, J, Q = 512, 512, 256, 512, 256, 128
FLOPS = 2 * C * D * Z + 2 * C * D * I + 2 * D * Q * Z

F32 = mybir.dt.float32
BF16 = mybir.dt.bfloat16
I32 = mybir.dt.int32
U32 = mybir.dt.uint32
U16 = mybir.dt.uint16
U8 = mybir.dt.uint8
FP8X4 = mybir.dt.float8_e4m3fn_x4
FP4X4 = mybir.dt.float4_e2m1fn_x4
COPY = mybir.ActivationFunctionType.Copy
ADD = mybir.AluOpType.add
SUBTRACT = mybir.AluOpType.subtract
MAX = mybir.AluOpType.max

mybir_bytes = {U32: 4, U16: 2, U8: 1}
P = 128
PACK = 4
QUADRANTS = 4
HALF = Z // 2
PIECES = 4
PIECE = Z // PIECES


def tile_attend_headturn_plainq_kernel(
    tc, wp_words, wp_scales, olds_words, olds_scales, wk_words, wk_scales, news_words, news_scales,
    query, sd, offs, offs2, offs3, offs4, out,
):
    nc = tc.nc
    with ExitStack() as ctx:
        sb = ctx.enter_context(tc.tile_pool(name="sb", bufs=1))
        ps = ctx.enter_context(tc.psum_pool(name="ps", bufs=1))

        def load_scale_rows(filler, name, scales, width):
            rows = sb.tile([P, 2, width], U8, name=name, align_bytes=64)
            filler.memset(rows[:].bitcast(I32), 0)
            by_quadrant = scales[0].rearrange("(h l r) c -> l r h c", h=2, l=2).bitcast(I32)
            for low in range(2):
                nc.sync.dma_start(rows[32 * low : 32 * low + 4].bitcast(I32), by_quadrant[low])
            return rows

        def complete_plane(rows):
            nc.vector.tensor_copy(rows[P // 2 :, 0, :].bitcast(I32), rows[: P // 2, 1, :].bitcast(I32))
            return rows[:, 0, :]

        def zeroed_plane(name, width):
            plane = sb.tile([P, width], U8, name=name, align_bytes=64)
            nc.vector.memset(plane[:].bitcast(I32), 0)
            return plane

        def spread(copy, plane, rows, u):
            copy(plane[32 * u : 32 * u + 4, :].bitcast(U32), rows[:, u, :])

        def deal(copy, dealt, given, first, last):
            run = 16 // mybir_bytes[given.dtype]
            copy(
                dealt.rearrange("p (t c i) -> p c t i", t=last - first, i=run),
                given.rearrange("p (c i t) -> p c t i", t=PACK, i=run)[:, :, first:last, :],
            )

        def load_list(name, source):
            offsets = sb.tile([P, source.shape[1]], U16, name=name)
            nc.sync.dma_start(offsets[:], source)
            return offsets

        wp_raw = sb.tile([P, D], U32, name="wp_raw")
        nc.sync.dma_start(wp_raw[:].bitcast(I32), wp_words[0].rearrange("p n t -> p (n t)").bitcast(I32))
        wp_rows = load_scale_rows(nc.gpsimd, "wp_rows", wp_scales, D)
        olds_codes = sb.tile([P, 2 * Z], U8, name="olds_codes", align_bytes=64)
        nc.sync.dma_start(olds_codes[:].bitcast(I32), olds_words[0].bitcast(I32))
        olds_rows = load_scale_rows(nc.vector, "olds_rows", olds_scales, Z)
        wk_rows = sb.tile([4, QUADRANTS, D // 4], U32, name="wk_rows")
        nc.sync.dma_start(wk_rows[:].bitcast(I32), wk_scales[0].rearrange("(u r) c -> r u c", r=4).bitcast(I32))
        wk_raw = sb.tile([P, 2 * D], U8, name="wk_raw")
        nc.sync.dma_start(wk_raw[:].bitcast(I32), wk_words[0].bitcast(I32))
        fetch_list = load_list("fetch_list", offs)
        sd_cols = sb.tile([P, PACK], F32, name="sd_cols")
        nc.sync.dma_start(sd_cols[:], sd.rearrange("(p t) o -> p (t o)", t=PACK))
        news_plane = zeroed_plane("news_plane", I)
        wk_spread = zeroed_plane("wk_spread", D)
        news_codes = sb.tile([P, I], U32, name="news_codes", align_bytes=64)
        nc.sync.dma_start(news_codes[:].bitcast(I32), news_words[0].rearrange("p n t -> p (n t)").bitcast(I32))
        for u in range(QUADRANTS):
            nc.sync.dma_start(
                news_plane[32 * u : 32 * u + 4, :].bitcast(I32), news_scales[0, 4 * u : 4 * u + 4, :].bitcast(I32)
            )
        put_list = load_list("put_list", offs2)
        pick_list_a = load_list("pick_list_a", offs3)
        pick_list_b = load_list("pick_list_b", offs4)

        f1 = [sb.tile([P, Z], F32, name="f1_%d" % t) for t in range(PACK)]
        for t in range(PACK):
            (nc.vector if t < 2 else nc.gpsimd).memset(f1[t][:], 0.0)

        wp_spread = complete_plane(wp_rows)
        olds_plane = complete_plane(olds_rows)
        wp_plane, wp_codes = [], []
        for first, last in ((0, 1), (1, PACK)):
            plane = sb.tile([P, P * (last - first)], U8, name="wp_plane_%d" % first, align_bytes=64)
            codes = sb.tile([P, P * (last - first)], U32, name="wp_codes_%d" % first, align_bytes=64)
            deal(nc.vector.tensor_copy, plane[:], wp_spread, first, last)
            deal(nc.scalar.copy, codes[:], wp_raw[:], first, last)
            wp_plane.extend(plane[:, P * n : P * (n + 1)] for n in range(last - first))
            wp_codes.extend(codes[:, P * n : P * (n + 1)] for n in range(last - first))

        query_raw = sb.tile([P, PACK, Q], F32, name="query_raw", tag="wp_raw")
        nc.sync.dma_start(query_raw[:], query.rearrange("(p t) q -> p t q", t=PACK))

        def kb_product(bank, t, z0, z1):
            nc.tensor.matmul_mx(
                out=bank,
                lhsT=wp_codes[t].bitcast(FP8X4),
                lhsT_scale=wp_plane[t],
                rhs=olds_codes[:, 2 * z0 : 2 * z1].bitcast(FP4X4),
                rhs_scale=olds_plane[:, z0:z1],
                start=True,
                stop=True,
            )

        kb = [sb.tile([P, Z], F32, name="kb_%d" % t) for t in range(PACK)]
        first_cuts = (0, HALF, HALF + PIECE, Z)
        first_banks = [ps.tile([P, z1 - z0], F32, name="kb_first_%d" % n) for n, (z0, z1) in enumerate(zip(first_cuts, first_cuts[1:]))]
        for bank, z0, z1 in zip(first_banks, first_cuts, first_cuts[1:]):
            kb_product(bank[:], 0, z0, z1)
        kb_banks = {t: ps.tile([P, Z], F32, name="kb_bank_%d" % t) for t in range(1, PACK)}
        for t in range(1, PACK):
            kb_product(kb_banks[t][:], t, 0, Z)

        wk_codes = sb.tile([P, 2 * D], U8, name="wk_codes", align_bytes=64)
        deal(nc.scalar.copy, wk_codes[:].bitcast(U16), wk_raw[:].bitcast(U16), 0, PACK)
        for copy, bank, z0, z1 in zip((nc.scalar.copy, nc.vector.tensor_copy, nc.vector.tensor_copy), first_banks, first_cuts, first_cuts[1:]):
            copy(kb[0][:, z0:z1], bank[:])
        for u in range(QUADRANTS):
            spread(nc.gpsimd.tensor_copy if u == 0 else nc.vector.tensor_copy, wk_spread, wk_rows, u)
        for t in range(1, PACK):
            nc.vector.tensor_copy(kb[t][:], kb_banks[t][:])
        wk_plane = sb.tile([P, D], U8, name="wk_plane", align_bytes=64)
        for t in range(PACK):
            deal(nc.gpsimd.tensor_copy, wk_plane[:, P * t : P * (t + 1)], wk_spread[:], t, t + 1)

        def kn_product(t):
            kn = ps.tile([P, I], F32, name="kn_%d" % t, tag="late_%d" % (t % 2))
            nc.tensor.matmul_mx(
                out=kn[:],
                lhsT=wk_codes[:, 2 * P * t : 2 * P * (t + 1)].bitcast(FP4X4),
                lhsT_scale=wk_plane[:, P * t : P * (t + 1)],
                rhs=news_codes[:].bitcast(FP8X4),
                rhs_scale=news_plane[:],
                start=True,
                stop=True,
            )
            return kn

        w = [sb.tile([P, I], F32, name="w_%d" % t) for t in range(PACK)]
        r = [sb.tile([P, I], F32, name="r_%d" % t) for t in range(PACK)]
        for t in range(PACK):
            nc.scalar.activation(w[t][:], kb[t][:].indirect(fetch_list[:]), COPY, scale=sd_cols[:, t : t + 1])
        for t in range(PACK):
            nc.vector.tensor_tensor(r[t][:], kn_product(t)[:], w[t][:], SUBTRACT)

        pg_pair = [sb.tile([P, 2, Z], BF16, name="pg_pair_%d" % u) for u in range(2)]
        pg = [sb.tile([P, PIECE, PACK], BF16, name="pg_%d" % k, align_bytes=64) for k in range(PIECES)]

        def put(t):
            nc.scalar.activation(f1[t][:].indirect(put_list[:]), r[t][:], COPY)

        def add(t, z0, z1):
            nc.vector.tensor_tensor(pg_pair[t // 2][:, t % 2, z0:z1], kb[t][:, z0:z1], f1[t][:, z0:z1], ADD)

        def weave(copy, u, k):
            copy(pg[k][:, :, 2 * u : 2 * u + 2], pg_pair[u][:, :, PIECE * k : PIECE * (k + 1)].rearrange("p e z -> p z e"))

        put(0)
        query_grouped = sb.tile([P, Q, PACK], BF16, name="query_grouped", align_bytes=64)
        nc.vector.tensor_copy(query_grouped[:], query_raw[:].rearrange("p t q -> p q t"))
        query_codes = sb.tile([P, Q], U32, name="query_codes", align_bytes=64)
        query_plane = sb.tile([P, Q], U8, name="query_plane", align_bytes=64)
        nc.vector.quantize_mx(
            query_codes[:].bitcast(FP8X4), query_plane[:], query_grouped[:].rearrange("p q t -> p (q t)")
        )
        add(0, 0, Z)
        put(1)
        add(1, 0, Z)
        for k in range(PIECES):
            weave(nc.vector.tensor_copy, 0, k)
        put(2)
        add(2, 0, Z)
        put(3)
        for k in (0, 2, 3, 1):
            add(3, PIECE * k, PIECE * (k + 1))
        for k in range(PIECES):
            weave(nc.scalar.copy if k < PIECES // 2 else nc.vector.tensor_copy, 1, k)

        s = sb.tile([P, Z], F32, name="s")
        s_banks = [ps.tile([P, PIECE], F32, name="s_bank_%d" % k, tag=tag) for k, tag in enumerate(("late_0", "late_1", "kb_first_0", "kb_first_1"))]
        order = (2, 0, 3, 1)
        for k in order:
            pg_codes = sb.tile([P, PIECE], U32, name="pg_codes_%d" % k, align_bytes=64)
            pg_plane = sb.tile([P, PIECE], U8, name="pg_plane_%d" % k, align_bytes=64)
            nc.vector.quantize_mx(pg_codes[:].bitcast(FP8X4), pg_plane[:], pg[k][:].rearrange("p z t -> p (z t)"))
            nc.tensor.matmul_mx(
                out=s_banks[k][:],
                lhsT=query_codes[:].bitcast(FP8X4),
                lhsT_scale=query_plane[:],
                rhs=pg_codes[:].bitcast(FP8X4),
                rhs_scale=pg_plane[:],
                start=True,
                stop=True,
            )
        for n, k in enumerate(order):
            copy = nc.scalar.copy if n < PIECES - 1 else nc.vector.tensor_copy
            copy(s[:, PIECE * k : PIECE * (k + 1)], s_banks[k][:])

        picked_a = sb.tile([P, J], F32, name="picked_a")
        picked_b = sb.tile([P, J], F32, name="picked_b")
        larger = sb.tile([P, J], F32, name="larger")
        halves = [(slice(J // 2 * h, J // 2 * (h + 1)), slice(J // 32 * h, J // 32 * (h + 1))) for h in range(2)]
        for picks, columns in halves:
            nc.scalar.activation(picked_a[:, picks], s[:].indirect(pick_list_a[:, columns]), COPY)
            nc.vector.tensor_copy(picked_b[:, picks], s[:].indirect(pick_list_b[:, columns]))
        for (picks, columns), queue in zip(halves, (nc.sync, nc.scalar)):
            nc.vector.tensor_tensor(larger[:, picks], picked_a[:, picks], picked_b[:, picks], MAX)
            queue.dma_start(out[:, picks], larger[:, picks])
